import numpy as np
import ml_dtypes


def mxq(x, axis, fmt="e4m3"):
    dtype, down = {"e4m3": (ml_dtypes.float8_e4m3fn, 7), "e5m2": (ml_dtypes.float8_e5m2, 14)}[fmt]
    v = np.moveaxis(np.asarray(x, np.float32).astype(ml_dtypes.bfloat16).astype(np.float64), axis, -1)
    blocks = v.reshape(v.shape[:-1] + (-1, 32))
    amax = np.abs(blocks).max(-1, keepdims=True)
    byte = np.maximum(np.where(amax > 0, np.frexp(amax)[1] - 1 + 127, 0) - down, 1)
    scale = np.exp2(byte - 127.0)
    codes = (blocks / scale).astype(np.float32).astype(dtype).astype(np.float64)
    return np.moveaxis((codes * scale).reshape(v.shape), -1, axis)


WIDE = False


def mx_kscale(k):
    if not WIDE:
        return np.ones(k)
    levels = np.array([10, -10, 5, -5, 0])
    if k % 512:
        return np.exp2(np.random.permutation(np.resize(levels, k // 32))).repeat(32)
    a = np.empty((k // 512, 16))
    for p in range(k // 512):
        a[p, :8] = np.random.permutation(np.resize(levels, 8))
        for g in range(8):
            far = levels[np.abs(levels - a[p, g]) >= 10]
            a[p, g + 8] = far[np.random.randint(len(far))]
    return np.exp2(a.ravel()).repeat(32)


def f64(x):
    return np.asarray(x).astype(np.float64)


E2M1 = np.array([0.0, 0.5, 1.0, 1.5, 2.0, 3.0, 4.0, 6.0, -0.0, -0.5, -1.0, -1.5, -2.0, -3.0, -4.0, -6.0])


def pack_weight(w, fmt):
    k, n = w.shape
    w = f64(np.asarray(w, np.float32).astype(ml_dtypes.bfloat16)).reshape(k // 32, 32, n)
    amax = np.abs(w).max(1)
    if fmt == "e4m3":
        byte = np.frexp(amax)[1] - 1 + 127 - 7
    else:
        mant, ex = np.frexp(amax / 6.0)
        byte = np.where(mant > 0.5, ex, ex - 1) + 127
    byte = np.clip(np.where(amax > 0, byte, 1), 1, 254)
    scaled = (w * np.exp2(127.0 - byte)[:, None, :]).reshape(k, n).astype(np.float32)
    by_word = np.ascontiguousarray(scaled.reshape(k // 512, 128, 4, n).transpose(0, 1, 3, 2))
    if fmt == "e4m3":
        words = by_word.astype(ml_dtypes.float8_e4m3fn).view(np.uint8)
    else:
        c = by_word.astype(ml_dtypes.float4_e2m1fn).view(np.uint8) & 0xF
        words = (c[..., 0::2] | (c[..., 1::2] << 4)).reshape(k // 512, 128, 2 * n)
    return np.ascontiguousarray(words), np.ascontiguousarray(byte.astype(np.uint8).reshape(k // 512, 16, n))


def unpack_weight(words, scales, fmt):
    g, _, n = scales.shape
    words = np.ascontiguousarray(words).reshape(g, 128, n, -1)
    if fmt == "e4m3":
        vals = words.view(ml_dtypes.float8_e4m3fn).astype(np.float64)
    else:
        nib = np.empty((g, 128, n, 4), np.uint8)
        nib[..., 0::2] = words & 0xF
        nib[..., 1::2] = words >> 4
        vals = E2M1[nib]
    vals = vals * np.repeat(np.exp2(scales.astype(np.float64) - 127.0), 8, axis=1)[..., None]
    return vals.transpose(0, 1, 3, 2).reshape(g * 512, n)


def bf(x):
    return np.asarray(x, np.float32).astype(ml_dtypes.bfloat16)


def planes(Y):
    r, m = Y.shape
    b = f64(bf(Y)).reshape(r // 32, 32, m)
    amax = np.abs(b).max(1)
    byte = np.clip(np.where(amax > 0, np.frexp(amax)[1] - 1 + 127 - 7, 1), 1, 254)
    codes = (b * np.exp2(127.0 - byte)[:, None, :]).reshape(r, m).astype(np.float32).astype(ml_dtypes.float8_e4m3fn).view(np.uint8)
    words = codes.reshape(r // 512, 128, 4, m).transpose(0, 1, 3, 2)
    return np.ascontiguousarray(words), np.ascontiguousarray(byte.astype(np.uint8).reshape(r // 512, 16, m))


K, L, T, N = 512, 1024, 512, 512


def setup_inputs():
    n = np.random.standard_normal
    fk = mx_kscale(K)
    fl = mx_kscale(L)
    wap = pack_weight(n((K, N)) * 1 / np.sqrt(K) * fk[:, None], "e2m1")
    xqp = pack_weight(n((L, T)) / fl[:, None], "e4m3")
    wqp = pack_weight(n((L, N)) * 1 / np.sqrt(L) * fl[:, None], "e2m1")
    wsp = pack_weight(n((L, N)) * 1 / np.sqrt(L) * fl[:, None], "e4m3")
    return {
        "xt": (n((K, T)) / fk[:, None]).astype(np.float32),
        "wa_words": wap[0],
        "wa_scales": wap[1],
        "xq_words": xqp[0],
        "xq_scales": xqp[1],
        "wq_words": wqp[0],
        "wq_scales": wqp[1],
        "wb": (n((K, N)) * 1 / np.sqrt(K) * fk[:, None]).astype(np.float32),
        "ws_words": wsp[0],
        "ws_scales": wsp[1],
    }


def reference(xt, wa_words, wa_scales, xq_words, xq_scales, wq_words, wq_scales, wb, ws_words, ws_scales):
    wau = unpack_weight(wa_words, wa_scales, "e2m1")
    xqu = unpack_weight(xq_words, xq_scales, "e4m3")
    wqu = unpack_weight(wq_words, wq_scales, "e2m1")
    wsu = unpack_weight(ws_words, ws_scales, "e4m3")
    xtq = mxq(f64(xt), 0, "e4m3")
    p = wau.T @ xtq + wqu.T @ xqu
    wbq = mxq(f64(wb), 0, "e4m3")
    r = wbq.T @ xtq + wsu.T @ xqu
    d = np.abs(p - r)
    y = np.maximum(p, r) + np.log(1.0 + np.exp(0.0 - d))
    words, scales = planes(y)
    return y, words, scales

@@ -1,0 +1,241 @@
+from contextlib import ExitStack
+
+import concourse.mybir as mybir
+from concourse.masks import make_identity
+
+K, L, T, N = 512, 1024, 512, 512
+FLOPS = 2 * 2 * (K + L) * N * T
+
+F32 = mybir.dt.float32
+BF16 = mybir.dt.bfloat16
+I32 = mybir.dt.int32
+U32 = mybir.dt.uint32
+U8 = mybir.dt.uint8
+FP8X4 = mybir.dt.float8_e4m3fn_x4
+FP4X4 = mybir.dt.float4_e2m1fn_x4
+ACT = mybir.ActivationFunctionType
+ALU = mybir.AluOpType
+
+P = 128
+PACK = 4
+TILES = T // P
+CAP = 24.0
+
+
+def tile_mix_smooth_larger_of_sums_pl_kernel(
+    tc, xt, wa_words, wa_scales, xq_words, xq_scales, wq_words, wq_scales, wb, ws_words, ws_scales,
+    out_0, out_1, out_2,
+):
+    nc = tc.nc
+    with ExitStack() as ctx:
+        sb = ctx.enter_context(tc.tile_pool(name="sb", bufs=1))
+        ps = ctx.enter_context(tc.psum_pool(name="ps", bufs=1))
+        ctx.enter_context(tc.manual_schedule())
+
+        def sbuf(name, shape, dtype):
+            return sb.tile(shape, dtype, name=name, align_bytes=64)
+
+        def plane(name, passes):
+            made = sbuf(name, [P, passes, 512], U8)
+            nc.vector.memset(made[:].bitcast(I32), 0)
+            return made
+
+        def load_scale_rows(queue, dst, src, quadrant):
+            queue.dma_start(
+                out=dst[32 * quadrant : 32 * quadrant + 4].bitcast(I32),
+                in_=src.rearrange("z q c -> q z c")[4 * quadrant : 4 * quadrant + 4].bitcast(I32),
+            )
+
+        def load_fp8(name, words):
+            made = sbuf(name, [P, 512], I32)
+            nc.sync.dma_start(out=made[:], in_=words.rearrange("p c r -> p (c r)").bitcast(I32))
+            return made
+
+        def load_rows(name, src, lo, width):
+            made = sbuf(name, [P, PACK, width], F32)
+            nc.sync.dma_start(out=made[:], in_=src.rearrange("(p j) c -> p j c", j=PACK)[:, :, lo : lo + width])
+            return made
+
+        def interleave(engine, dst, src):
+            o = dst.rearrange("p (c i) j -> p c j i", i=4)
+            s = src.rearrange("p j (c i) -> p c j i", i=4)
+            if engine == "vector":
+                nc.vector.tensor_copy(out=o, in_=s)
+            else:
+                nc.scalar.copy(out=o, in_=s)
+
+        def quantize(codes, scales, grouped):
+            nc.vector.quantize_mx(out=codes.bitcast(FP8X4), scales=scales, in_=grouped.rearrange("p c j -> p (c j)"))
+
+        xq_sc = plane("xq_sc", 2)
+        wq_sc = plane("wq_sc", 2)
+        wa_sc = plane("wa_sc", 1)
+        ws_sc = plane("ws_sc", 2)
+
+        for q in range(4):
+            load_scale_rows(nc.gpsimd, wa_sc, wa_scales, q)
+        xq = [None, None]
+        xq[0] = load_fp8("xq0", xq_words[0])
+        wq = sbuf("wq", [P, 2, 1024], U8)
+        nc.sync.dma_start(out=wq[:].bitcast(I32), in_=wq_words.rearrange("z p c -> p z c").bitcast(I32))
+        for q in range(4):
+            load_scale_rows(nc.sync, xq_sc, xq_scales, q)
+        load_scale_rows(nc.sync, wq_sc, wq_scales, 0)
+        xq[1] = load_fp8("xq1", xq_words[1])
+        for q in range(1, 4):
+            load_scale_rows(nc.sync, wq_sc, wq_scales, q)
+        ws = sbuf("ws", [P, 2, 512], I32)
+        nc.sync.dma_start(out=ws[:], in_=ws_words.rearrange("z p c r -> p z (c r)").bitcast(I32))
+        xt_spans = [(0, 256), (256, 128), (384, 128)]
+        xt_raw = [None] * 3
+        xt_raw[0] = load_rows("xt_raw0", xt, 0, 256)
+        for q in range(4):
+            load_scale_rows(nc.sync, ws_sc, ws_scales, q)
+        wa = sbuf("wa", [P, 1024], U8)
+        nc.sync.dma_start(out=wa[:].bitcast(I32), in_=wa_words[0].bitcast(I32))
+        wb_raw = [load_rows("wb_raw%d" % h, wb, 256 * h, 256) for h in range(2)]
+        xt_raw[1] = load_rows("xt_raw1", xt, 256, 128)
+        xt_raw[2] = load_rows("xt_raw2", xt, 384, 128)
+
+        ident = sbuf("ident", [P, P], F32)
+        make_identity(nc, ident[:])
+
+        xt_codes = [sbuf("xt_codes%d" % c, [P, w], U32) for c, (lo, w) in enumerate(xt_spans)]
+        xt_sc = [sbuf("xt_sc%d" % c, [P, w], U8) for c, (lo, w) in enumerate(xt_spans)]
+        xt_bf = [sbuf("xt_bf%d" % c, [P, w, PACK], BF16) for c, (lo, w) in enumerate(xt_spans)]
+        wb_codes = sbuf("wb_codes", [P, 512], U32)
+        wb_sc = sbuf("wb_sc", [P, 512], U8)
+        wb_bf = [sbuf("wb_bf%d" % h, [P, 256, PACK], BF16) for h in range(2)]
+
+        interleave("vector", xt_bf[0][:], xt_raw[0][:])
+        quantize(xt_codes[0][:], xt_sc[0][:], xt_bf[0][:])
+        interleave("vector", wb_bf[0][:], wb_raw[0][:])
+        quantize(wb_codes[:, 0:256], wb_sc[:, 0:256], wb_bf[0][:])
+        interleave("scalar", wb_bf[1][:, 0:128], wb_raw[1][:, :, 0:128])
+        interleave("vector", wb_bf[1][:, 128:256], wb_raw[1][:, :, 128:256])
+        quantize(wb_codes[:, 256:512], wb_sc[:, 256:512], wb_bf[1][:])
+        for c in (1, 2):
+            interleave("vector", xt_bf[c][:], xt_raw[c][:])
+            quantize(xt_codes[c][:], xt_sc[c][:], xt_bf[c][:])
+
+        def xt_tile(i):
+            c, lo = (0, P * i) if i < 2 else (i - 1, 0)
+            return xt_codes[c][:, lo : lo + P].bitcast(FP8X4), xt_sc[c][:, lo : lo + P]
+
+        first = [ps.tile([P, 512], F32, name="first%d" % i) for i in range(TILES)]
+        second = [ps.tile([P, 512], F32, name="second%d" % i) for i in range(TILES)]
+
+        def l_pass(bank, i, z, rhs, rhs_scale):
+            cols = slice(P * i, P * (i + 1))
+            nc.tensor.matmul_mx(
+                out=bank[:], lhsT=xq[z][:, cols].bitcast(FP8X4), lhsT_scale=xq_sc[:, z, cols],
+                rhs=rhs, rhs_scale=rhs_scale, start=(z == 0), stop=False,
+            )
+
+        def k_pass(bank, i, rhs, rhs_scale):
+            codes, scales = xt_tile(i)
+            nc.tensor.matmul_mx(out=bank[:], lhsT=codes, lhsT_scale=scales, rhs=rhs, rhs_scale=rhs_scale, start=False, stop=True)
+
+        def close_first(i):
+            k_pass(first[i], i, wa[:].bitcast(FP4X4), wa_sc[:, 0, :])
+
+        def close_second(i):
+            k_pass(second[i], i, wb_codes[:].bitcast(FP8X4), wb_sc[:])
+
+        p_sb = [sbuf("p_sb%d" % i, [P, PACK, P], F32) for i in range(TILES)]
+        gap = [sbuf("gap%d" % i, [P, PACK, P], F32) for i in range(TILES)]
+        low = [sbuf("low%d" % i, [P, PACK, P], F32) for i in range(TILES)]
+        high = [sbuf("high%d" % i, [P, PACK, P], F32) for i in range(TILES)]
+        grown = [sbuf("grown%d" % i, [P, PACK, P], F32) for i in range(TILES)]
+        soft = [sbuf("soft%d" % i, [P, PACK, P], F32) for i in range(TILES)]
+        y = [sbuf("y%d" % i, [P, PACK, P], F32) for i in range(TILES)]
+
+        def dealt(bank):
+            return bank[:].rearrange("t (m r) -> t r m", r=PACK)
+
+        def copy_first(i):
+            nc.scalar.copy(out=p_sb[i][:], in_=dealt(first[i]))
+
+        def sub(i):
+            nc.vector.tensor_tensor(out=gap[i][:], in0=dealt(second[i]), in1=p_sb[i][:], op=ALU.subtract)
+
+        def clip(i):
+            nc.vector.tensor_scalar(out=low[i][:], in0=gap[i][:], scalar1=CAP, scalar2=None, op0=ALU.min)
+
+        def rest(i):
+            nc.vector.tensor_scalar(out=high[i][:], in0=gap[i][:], scalar1=CAP, scalar2=0.0, op0=ALU.subtract, op1=ALU.max)
+
+        def exp(i):
+            nc.scalar.activation(out=grown[i][:], in_=low[i][:], func=ACT.Exp)
+
+        def log(i):
+            nc.scalar.activation(out=soft[i][:], in_=grown[i][:], func=ACT.Ln, bias=1.0)
+
+        def turn(i, term, opens, closes):
+            for r in range(PACK):
+                nc.tensor.matmul(
+                    out=first[i][:, P * r : P * (r + 1)], lhsT=term[i][:, r, :], rhs=ident[:], is_transpose=True,
+                    start=(opens and r == 0), stop=(closes and r == PACK - 1),
+                )
+
+        for z in range(2):
+            for i in range(TILES):
+                l_pass(first[i], i, z, wq[:, z, :].bitcast(FP4X4), wq_sc[:, z, :])
+        for i in range(TILES):
+            l_pass(second[i], i, 0, ws[:, 0, :].bitcast(FP8X4), ws_sc[:, 0, :])
+        for i in (0, 1):
+            close_first(i)
+            copy_first(i)
+        for i in range(TILES):
+            l_pass(second[i], i, 1, ws[:, 1, :].bitcast(FP8X4), ws_sc[:, 1, :])
+        for i in (0, 1):
+            close_second(i)
+        for i in (2, 3):
+            close_first(i)
+            close_second(i)
+            copy_first(i)
+
+        for pair in ((0, 1), (2, 3)):
+            for i in pair:
+                sub(i)
+            for i in pair:
+                clip(i)
+        for i in range(TILES):
+            exp(i)
+        for i in range(TILES):
+            turn(i, p_sb, True, False)
+        for i in range(TILES):
+            rest(i)
+            turn(i, high, False, False)
+        for i in range(TILES):
+            log(i)
+            turn(i, soft, False, True)
+
+        y_bf = [sbuf("y_bf0", [P, 256, PACK], BF16), sbuf("y_bf1", [P, P, PACK], BF16), sbuf("y_bf2", [P, P, PACK], BF16)]
+        y_codes = sbuf("y_codes", [P, 512], U32)
+        y_sc = sbuf("y_sc", [P, 512], U8)
+        out_rows = out_0.rearrange("(p r) t -> p r t", r=PACK)
+        out_words = out_1[0].rearrange("p c r -> p (c r)").bitcast(I32)
+
+        for i in range(TILES):
+            src = first[i][:].rearrange("p (r t) -> p r t", r=PACK)
+            if i < 2:
+                nc.vector.tensor_copy(out=y[i][:], in_=src)
+            else:
+                nc.scalar.copy(out=y[i][:], in_=src)
+            nc.sync.dma_start(out=out_rows[:, :, P * i : P * (i + 1)], in_=y[i][:])
+        interleave("vector", y_bf[0][:, 0:P], y[0][:])
+        interleave("vector", y_bf[0][:, P : 2 * P], y[1][:])
+        interleave("vector", y_bf[1][:], y[2][:])
+        quantize(y_codes[:, 0:256], y_sc[:, 0:256], y_bf[0][:])
+        nc.sync.dma_start(out=out_words[:, 0:256], in_=y_codes[:, 0:256].bitcast(I32))
+        interleave("vector", y_bf[2][:], y[3][:])
+        quantize(y_codes[:, 256:384], y_sc[:, 256:384], y_bf[1][:])
+        quantize(y_codes[:, 384:512], y_sc[:, 384:512], y_bf[2][:])
+        nc.sync.dma_start(out=out_words[:, 256:512], in_=y_codes[:, 256:512].bitcast(I32))
+        for q in range(4):
+            queue = nc.scalar if q < 2 else nc.sync
+            queue.dma_start(
+                out=out_2[0, 4 * q : 4 * q + 4, :].bitcast(I32),
+                in_=y_sc[32 * q : 32 * q + 4, :].bitcast(I32),
+            )

@@ -20,6 +20,7 @@ P = 128
 PACK = 4
 TILES = T // P
 CAP = 24.0
+CLIPPED_ON_SCALAR = (0, 1)
 
 
 def tile_mix_smooth_larger_of_sums_pl_kernel(
@@ -35,9 +36,9 @@ def tile_mix_smooth_larger_of_sums_pl_kernel(
         def sbuf(name, shape, dtype):
             return sb.tile(shape, dtype, name=name, align_bytes=64)
 
-        def plane(name, passes):
+        def plane(name, passes, engine):
             made = sbuf(name, [P, passes, 512], U8)
-            nc.vector.memset(made[:].bitcast(I32), 0)
+            engine.memset(made[:].bitcast(I32), 0)
             return made
 
         def load_scale_rows(queue, dst, src, quadrant):
@@ -67,10 +68,10 @@ def tile_mix_smooth_larger_of_sums_pl_kernel(
         def quantize(codes, scales, grouped):
             nc.vector.quantize_mx(out=codes.bitcast(FP8X4), scales=scales, in_=grouped.rearrange("p c j -> p (c j)"))
 
-        xq_sc = plane("xq_sc", 2)
-        wq_sc = plane("wq_sc", 2)
-        wa_sc = plane("wa_sc", 1)
-        ws_sc = plane("ws_sc", 2)
+        xq_sc = plane("xq_sc", 2, nc.vector)
+        wq_sc = plane("wq_sc", 2, nc.vector)
+        wa_sc = plane("wa_sc", 1, nc.gpsimd)
+        ws_sc = plane("ws_sc", 2, nc.vector)
 
         for q in range(4):
             load_scale_rows(nc.gpsimd, wa_sc, wa_scales, q)
@@ -81,46 +82,42 @@ def tile_mix_smooth_larger_of_sums_pl_kernel(
         for q in range(4):
             load_scale_rows(nc.sync, xq_sc, xq_scales, q)
         load_scale_rows(nc.sync, wq_sc, wq_scales, 0)
-        xq[1] = load_fp8("xq1", xq_words[1])
-        for q in range(1, 4):
-            load_scale_rows(nc.sync, wq_sc, wq_scales, q)
         ws = sbuf("ws", [P, 2, 512], I32)
         nc.sync.dma_start(out=ws[:], in_=ws_words.rearrange("z p c r -> p z (c r)").bitcast(I32))
-        xt_spans = [(0, 256), (256, 128), (384, 128)]
-        xt_raw = [None] * 3
-        xt_raw[0] = load_rows("xt_raw0", xt, 0, 256)
+        for q in range(1, 4):
+            load_scale_rows(nc.sync, wq_sc, wq_scales, q)
+        xq[1] = load_fp8("xq1", xq_words[1])
         for q in range(4):
             load_scale_rows(nc.sync, ws_sc, ws_scales, q)
+        xt_raw = load_rows("xt_raw", xt, 0, 512)
         wa = sbuf("wa", [P, 1024], U8)
         nc.sync.dma_start(out=wa[:].bitcast(I32), in_=wa_words[0].bitcast(I32))
-        wb_raw = [load_rows("wb_raw%d" % h, wb, 256 * h, 256) for h in range(2)]
-        xt_raw[1] = load_rows("xt_raw1", xt, 256, 128)
-        xt_raw[2] = load_rows("xt_raw2", xt, 384, 128)
+        wb_spans = [(0, 256), (256, 128), (384, 128)]
+        wb_raw = [load_rows("wb_raw%d" % c, wb, lo, w) for c, (lo, w) in enumerate(wb_spans)]
 
         ident = sbuf("ident", [P, P], F32)
         make_identity(nc, ident[:])
+        cap_col = sbuf("cap_col", [P, 1], F32)
+        nc.gpsimd.memset(cap_col[:], CAP)
 
-        xt_codes = [sbuf("xt_codes%d" % c, [P, w], U32) for c, (lo, w) in enumerate(xt_spans)]
-        xt_sc = [sbuf("xt_sc%d" % c, [P, w], U8) for c, (lo, w) in enumerate(xt_spans)]
-        xt_bf = [sbuf("xt_bf%d" % c, [P, w, PACK], BF16) for c, (lo, w) in enumerate(xt_spans)]
-        wb_codes = sbuf("wb_codes", [P, 512], U32)
-        wb_sc = sbuf("wb_sc", [P, 512], U8)
-        wb_bf = [sbuf("wb_bf%d" % h, [P, 256, PACK], BF16) for h in range(2)]
+        xt_codes = [sbuf("xt_codes%d" % h, [P, 256], U32) for h in range(2)]
+        xt_sc = [sbuf("xt_sc%d" % h, [P, 256], U8) for h in range(2)]
+        xt_bf = [sbuf("xt_bf%d" % h, [P, 256, PACK], BF16) for h in range(2)]
+        wb_codes = [sbuf("wb_codes%d" % c, [P, w], U32) for c, (lo, w) in enumerate(wb_spans)]
+        wb_sc = [sbuf("wb_sc%d" % c, [P, w], U8) for c, (lo, w) in enumerate(wb_spans)]
+        wb_bf = [sbuf("wb_bf%d" % c, [P, w, PACK], BF16) for c, (lo, w) in enumerate(wb_spans)]
 
-        interleave("vector", xt_bf[0][:], xt_raw[0][:])
-        quantize(xt_codes[0][:], xt_sc[0][:], xt_bf[0][:])
-        interleave("vector", wb_bf[0][:], wb_raw[0][:])
-        quantize(wb_codes[:, 0:256], wb_sc[:, 0:256], wb_bf[0][:])
-        interleave("scalar", wb_bf[1][:, 0:128], wb_raw[1][:, :, 0:128])
-        interleave("vector", wb_bf[1][:, 128:256], wb_raw[1][:, :, 128:256])
-        quantize(wb_codes[:, 256:512], wb_sc[:, 256:512], wb_bf[1][:])
-        for c in (1, 2):
-            interleave("vector", xt_bf[c][:], xt_raw[c][:])
-            quantize(xt_codes[c][:], xt_sc[c][:], xt_bf[c][:])
+        interleave("vector", xt_bf[0][:], xt_raw[:, :, 0:256])
+        interleave("scalar", xt_bf[1][:], xt_raw[:, :, 256:512])
+        for h in range(2):
+            quantize(xt_codes[h][:], xt_sc[h][:], xt_bf[h][:])
+        for c in range(3):
+            interleave("vector", wb_bf[c][:], wb_raw[c][:])
+            quantize(wb_codes[c][:], wb_sc[c][:], wb_bf[c][:])
 
         def xt_tile(i):
-            c, lo = (0, P * i) if i < 2 else (i - 1, 0)
-            return xt_codes[c][:, lo : lo + P].bitcast(FP8X4), xt_sc[c][:, lo : lo + P]
+            h, lo = i // 2, P * (i % 2)
+            return xt_codes[h][:, lo : lo + P].bitcast(FP8X4), xt_sc[h][:, lo : lo + P]
 
         first = [ps.tile([P, 512], F32, name="first%d" % i) for i in range(TILES)]
         second = [ps.tile([P, 512], F32, name="second%d" % i) for i in range(TILES)]
@@ -132,15 +129,20 @@ def tile_mix_smooth_larger_of_sums_pl_kernel(
                 rhs=rhs, rhs_scale=rhs_scale, start=(z == 0), stop=False,
             )
 
-        def k_pass(bank, i, rhs, rhs_scale):
-            codes, scales = xt_tile(i)
-            nc.tensor.matmul_mx(out=bank[:], lhsT=codes, lhsT_scale=scales, rhs=rhs, rhs_scale=rhs_scale, start=False, stop=True)
-
         def close_first(i):
-            k_pass(first[i], i, wa[:].bitcast(FP4X4), wa_sc[:, 0, :])
+            codes, scales = xt_tile(i)
+            nc.tensor.matmul_mx(
+                out=first[i][:], lhsT=codes, lhsT_scale=scales, rhs=wa[:].bitcast(FP4X4), rhs_scale=wa_sc[:, 0, :],
+                start=False, stop=True,
+            )
 
-        def close_second(i):
-            k_pass(second[i], i, wb_codes[:].bitcast(FP8X4), wb_sc[:])
+        def wb_pass(i, c):
+            codes, scales = xt_tile(i)
+            lo, w = wb_spans[c]
+            nc.tensor.matmul_mx(
+                out=second[i][:, lo : lo + w], lhsT=codes, lhsT_scale=scales,
+                rhs=wb_codes[c][:].bitcast(FP8X4), rhs_scale=wb_sc[c][:], start=False, stop=(c == 2),
+            )
 
         p_sb = [sbuf("p_sb%d" % i, [P, PACK, P], F32) for i in range(TILES)]
         gap = [sbuf("gap%d" % i, [P, PACK, P], F32) for i in range(TILES)]
@@ -160,13 +162,21 @@ def tile_mix_smooth_larger_of_sums_pl_kernel(
             nc.vector.tensor_tensor(out=gap[i][:], in0=dealt(second[i]), in1=p_sb[i][:], op=ALU.subtract)
 
         def clip(i):
-            nc.vector.tensor_scalar(out=low[i][:], in0=gap[i][:], scalar1=CAP, scalar2=None, op0=ALU.min)
+            if i in CLIPPED_ON_SCALAR:
+                nc.scalar.activation(out=low[i][:], in_=gap[i][:], func=ACT.Relu, scale=-1.0, bias=cap_col[:])
+            else:
+                nc.vector.tensor_scalar(out=low[i][:], in0=gap[i][:], scalar1=CAP, scalar2=None, op0=ALU.min)
 
         def rest(i):
-            nc.vector.tensor_scalar(out=high[i][:], in0=gap[i][:], scalar1=CAP, scalar2=0.0, op0=ALU.subtract, op1=ALU.max)
+            nc.vector.scalar_tensor_tensor(
+                out=high[i][:], in0=dealt(second[i]), scalar=CAP, in1=p_sb[i][:], op0=ALU.subtract, op1=ALU.max
+            )
 
         def exp(i):
-            nc.scalar.activation(out=grown[i][:], in_=low[i][:], func=ACT.Exp)
+            if i in CLIPPED_ON_SCALAR:
+                nc.scalar.activation(out=grown[i][:], in_=low[i][:], func=ACT.Exp, scale=-1.0, bias=cap_col[:])
+            else:
+                nc.scalar.activation(out=grown[i][:], in_=low[i][:], func=ACT.Exp)
 
         def log(i):
             nc.scalar.activation(out=soft[i][:], in_=grown[i][:], func=ACT.Ln, bias=1.0)
@@ -183,30 +193,26 @@ def tile_mix_smooth_larger_of_sums_pl_kernel(
                 l_pass(first[i], i, z, wq[:, z, :].bitcast(FP4X4), wq_sc[:, z, :])
         for i in range(TILES):
             l_pass(second[i], i, 0, ws[:, 0, :].bitcast(FP8X4), ws_sc[:, 0, :])
-        for i in (0, 1):
+        for i in range(TILES):
+            l_pass(second[i], i, 1, ws[:, 1, :].bitcast(FP8X4), ws_sc[:, 1, :])
+        for i in range(TILES):
             close_first(i)
             copy_first(i)
         for i in range(TILES):
-            l_pass(second[i], i, 1, ws[:, 1, :].bitcast(FP8X4), ws_sc[:, 1, :])
-        for i in (0, 1):
-            close_second(i)
-        for i in (2, 3):
-            close_first(i)
-            close_second(i)
-            copy_first(i)
+            wb_pass(i, 0)
+        for i in range(TILES):
+            wb_pass(i, 1)
+            wb_pass(i, 2)
 
-        for pair in ((0, 1), (2, 3)):
-            for i in pair:
-                sub(i)
-            for i in pair:
-                clip(i)
+        for i in range(TILES):
+            sub(i)
+        for i in range(TILES):
+            clip(i)
         for i in range(TILES):
             exp(i)
         for i in range(TILES):
-            turn(i, p_sb, True, False)
-        for i in range(TILES):
             rest(i)
-            turn(i, high, False, False)
+            turn(i, high, True, False)
         for i in range(TILES):
             log(i)
             turn(i, soft, False, True)

@@ -20,6 +20,7 @@ P = 128
 PACK = 4
 TILES = T // P
 CAP = 24.0
+WARM_PASSES = 22
 CLIPPED_ON_SCALAR = (0, 1)
 
 
@@ -70,30 +71,37 @@ def tile_mix_smooth_larger_of_sums_pl_kernel(
 
         xq_sc = plane("xq_sc", 2, nc.vector)
         wq_sc = plane("wq_sc", 2, nc.vector)
-        wa_sc = plane("wa_sc", 1, nc.gpsimd)
+        warm_bf = sbuf("warm_bf", [P, P, PACK], BF16)
+        warm_codes = sbuf("warm_codes", [P, P], U32)
+        warm_sc = sbuf("warm_sc", [P, P], U8)
+        nc.vector.memset(warm_bf[:], 1.0)
         ws_sc = plane("ws_sc", 2, nc.vector)
+        wa_sc = plane("wa_sc", 1, nc.vector)
+        quantize(warm_codes[:], warm_sc[:], warm_bf[:])
 
-        for q in range(4):
-            load_scale_rows(nc.gpsimd, wa_sc, wa_scales, q)
         xq = [None, None]
-        xq[0] = load_fp8("xq0", xq_words[0])
         wq = sbuf("wq", [P, 2, 1024], U8)
         nc.sync.dma_start(out=wq[:].bitcast(I32), in_=wq_words.rearrange("z p c -> p z c").bitcast(I32))
+        xq[0] = load_fp8("xq0", xq_words[0])
         for q in range(4):
             load_scale_rows(nc.sync, xq_sc, xq_scales, q)
         load_scale_rows(nc.sync, wq_sc, wq_scales, 0)
-        ws = sbuf("ws", [P, 2, 512], I32)
-        nc.sync.dma_start(out=ws[:], in_=ws_words.rearrange("z p c r -> p z (c r)").bitcast(I32))
+        xt_raw = load_rows("xt_raw", xt, 0, 512)
         for q in range(1, 4):
             load_scale_rows(nc.sync, wq_sc, wq_scales, q)
         xq[1] = load_fp8("xq1", xq_words[1])
-        for q in range(4):
-            load_scale_rows(nc.sync, ws_sc, ws_scales, q)
-        xt_raw = load_rows("xt_raw", xt, 0, 512)
         wa = sbuf("wa", [P, 1024], U8)
         nc.sync.dma_start(out=wa[:].bitcast(I32), in_=wa_words[0].bitcast(I32))
-        wb_spans = [(0, 256), (256, 128), (384, 128)]
-        wb_raw = [load_rows("wb_raw%d" % c, wb, lo, w) for c, (lo, w) in enumerate(wb_spans)]
+        wb_raw = [None, None]
+        wb_raw[0] = load_rows("wb_raw0", wb, 0, 256)
+        for q in range(4):
+            load_scale_rows(nc.sync, wa_sc, wa_scales, q)
+        wb_raw[1] = load_rows("wb_raw1", wb, 256, 256)
+        ws = sbuf("ws", [P, 2, 512], I32)
+        nc.sync.dma_start(out=ws[:], in_=ws_words.rearrange("z p c r -> p z (c r)").bitcast(I32))
+        for q in range(4):
+            load_scale_rows(nc.sync, ws_sc, ws_scales, q)
+        wb_spans = [(0, 256), (256, 256)]
 
         ident = sbuf("ident", [P, P], F32)
         make_identity(nc, ident[:])
@@ -111,9 +119,8 @@ def tile_mix_smooth_larger_of_sums_pl_kernel(
         interleave("scalar", xt_bf[1][:], xt_raw[:, :, 256:512])
         for h in range(2):
             quantize(xt_codes[h][:], xt_sc[h][:], xt_bf[h][:])
-        for c in range(3):
-            interleave("vector", wb_bf[c][:], wb_raw[c][:])
-            quantize(wb_codes[c][:], wb_sc[c][:], wb_bf[c][:])
+        interleave("vector", wb_bf[0][:], wb_raw[0][:])
+        quantize(wb_codes[0][:], wb_sc[0][:], wb_bf[0][:])
 
         def xt_tile(i):
             h, lo = i // 2, P * (i % 2)
@@ -122,11 +129,11 @@ def tile_mix_smooth_larger_of_sums_pl_kernel(
         first = [ps.tile([P, 512], F32, name="first%d" % i) for i in range(TILES)]
         second = [ps.tile([P, 512], F32, name="second%d" % i) for i in range(TILES)]
 
-        def l_pass(bank, i, z, rhs, rhs_scale):
+        def l_pass(bank, i, z, rhs, rhs_scale, start, stop):
             cols = slice(P * i, P * (i + 1))
             nc.tensor.matmul_mx(
                 out=bank[:], lhsT=xq[z][:, cols].bitcast(FP8X4), lhsT_scale=xq_sc[:, z, cols],
-                rhs=rhs, rhs_scale=rhs_scale, start=(z == 0), stop=False,
+                rhs=rhs, rhs_scale=rhs_scale, start=start, stop=stop,
             )
 
         def close_first(i):
@@ -141,7 +148,7 @@ def tile_mix_smooth_larger_of_sums_pl_kernel(
             lo, w = wb_spans[c]
             nc.tensor.matmul_mx(
                 out=second[i][:, lo : lo + w], lhsT=codes, lhsT_scale=scales,
-                rhs=wb_codes[c][:].bitcast(FP8X4), rhs_scale=wb_sc[c][:], start=False, stop=(c == 2),
+                rhs=wb_codes[c][:].bitcast(FP8X4), rhs_scale=wb_sc[c][:], start=(c == 0), stop=False,
             )
 
         p_sb = [sbuf("p_sb%d" % i, [P, PACK, P], F32) for i in range(TILES)]
@@ -188,21 +195,28 @@ def tile_mix_smooth_larger_of_sums_pl_kernel(
                     start=(opens and r == 0), stop=(closes and r == PACK - 1),
                 )
 
+        for rep in range(WARM_PASSES):
+            nc.tensor.matmul_mx(
+                out=second[3][:, 0:P], lhsT=warm_codes[:].bitcast(FP8X4), lhsT_scale=warm_sc[:],
+                rhs=warm_codes[:].bitcast(FP8X4), rhs_scale=warm_sc[:], start=True, stop=True,
+            )
         for z in range(2):
             for i in range(TILES):
-                l_pass(first[i], i, z, wq[:, z, :].bitcast(FP4X4), wq_sc[:, z, :])
-        for i in range(TILES):
-            l_pass(second[i], i, 0, ws[:, 0, :].bitcast(FP8X4), ws_sc[:, 0, :])
-        for i in range(TILES):
-            l_pass(second[i], i, 1, ws[:, 1, :].bitcast(FP8X4), ws_sc[:, 1, :])
+                l_pass(first[i], i, z, wq[:, z, :].bitcast(FP4X4), wq_sc[:, z, :], z == 0, False)
         for i in range(TILES):
             close_first(i)
+        copy_first(0)
+        interleave("scalar", wb_bf[1][:, 0:96], wb_raw[1][:, :, 0:96])
+        interleave("vector", wb_bf[1][:, 96:256], wb_raw[1][:, :, 96:256])
+        quantize(wb_codes[1][:], wb_sc[1][:], wb_bf[1][:])
+        for i in range(1, TILES):
             copy_first(i)
         for i in range(TILES):
             wb_pass(i, 0)
         for i in range(TILES):
             wb_pass(i, 1)
-            wb_pass(i, 2)
+            for z in range(2):
+                l_pass(second[i], i, z, ws[:, z, :].bitcast(FP8X4), ws_sc[:, z, :], False, z == 1)
 
         for i in range(TILES):
             sub(i)

@@ -20,7 +20,8 @@ P = 128
 PACK = 4
 TILES = T // P
 CAP = 24.0
-WARM_PASSES = 22
+WARM_PASSES = 30
+KEEP_PASSES = 6
 CLIPPED_ON_SCALAR = (0, 1)
 
 
@@ -205,11 +206,10 @@ def tile_mix_smooth_larger_of_sums_pl_kernel(
                 l_pass(first[i], i, z, wq[:, z, :].bitcast(FP4X4), wq_sc[:, z, :], z == 0, False)
         for i in range(TILES):
             close_first(i)
-        copy_first(0)
         interleave("scalar", wb_bf[1][:, 0:96], wb_raw[1][:, :, 0:96])
         interleave("vector", wb_bf[1][:, 96:256], wb_raw[1][:, :, 96:256])
         quantize(wb_codes[1][:], wb_sc[1][:], wb_bf[1][:])
-        for i in range(1, TILES):
+        for i in range(TILES):
             copy_first(i)
         for i in range(TILES):
             wb_pass(i, 0)
@@ -217,6 +217,9 @@ def tile_mix_smooth_larger_of_sums_pl_kernel(
             wb_pass(i, 1)
             for z in range(2):
                 l_pass(second[i], i, z, ws[:, z, :].bitcast(FP8X4), ws_sc[:, z, :], False, z == 1)
+
+        for rep in range(KEEP_PASSES):
+            l_pass(first[3], 3, 1, ws[:, 1, :].bitcast(FP8X4), ws_sc[:, 1, :], True, True)
 
         for i in range(TILES):
             sub(i)

from contextlib import ExitStack

import concourse.mybir as mybir
from concourse.masks import make_identity

K, L, T, N = 512, 1024, 512, 512
FLOPS = 2 * 2 * (K + L) * N * T

F32 = mybir.dt.float32
BF16 = mybir.dt.bfloat16
I32 = mybir.dt.int32
U32 = mybir.dt.uint32
U8 = mybir.dt.uint8
FP8X4 = mybir.dt.float8_e4m3fn_x4
FP4X4 = mybir.dt.float4_e2m1fn_x4
ACT = mybir.ActivationFunctionType
ALU = mybir.AluOpType

P = 128
PACK = 4
TILES = T // P
CAP = 24.0
WARM_PASSES = 30
KEEP_PASSES = 6
CLIPPED_ON_SCALAR = (0, 1)


def tile_mix_smooth_larger_of_sums_pl_kernel(
    tc, xt, wa_words, wa_scales, xq_words, xq_scales, wq_words, wq_scales, wb, ws_words, ws_scales,
    out_0, out_1, out_2,
):
    nc = tc.nc
    with ExitStack() as ctx:
        sb = ctx.enter_context(tc.tile_pool(name="sb", bufs=1))
        ps = ctx.enter_context(tc.psum_pool(name="ps", bufs=1))
        ctx.enter_context(tc.manual_schedule())

        def sbuf(name, shape, dtype):
            return sb.tile(shape, dtype, name=name, align_bytes=64)

        def plane(name, passes, engine):
            made = sbuf(name, [P, passes, 512], U8)
            engine.memset(made[:].bitcast(I32), 0)
            return made

        def load_scale_rows(queue, dst, src, quadrant):
            queue.dma_start(
                out=dst[32 * quadrant : 32 * quadrant + 4].bitcast(I32),
                in_=src.rearrange("z q c -> q z c")[4 * quadrant : 4 * quadrant + 4].bitcast(I32),
            )

        def load_fp8(name, words):
            made = sbuf(name, [P, 512], I32)
            nc.sync.dma_start(out=made[:], in_=words.rearrange("p c r -> p (c r)").bitcast(I32))
            return made

        def load_rows(name, src, lo, width):
            made = sbuf(name, [P, PACK, width], F32)
            nc.sync.dma_start(out=made[:], in_=src.rearrange("(p j) c -> p j c", j=PACK)[:, :, lo : lo + width])
            return made

        def interleave(engine, dst, src):
            o = dst.rearrange("p (c i) j -> p c j i", i=4)
            s = src.rearrange("p j (c i) -> p c j i", i=4)
            if engine == "vector":
                nc.vector.tensor_copy(out=o, in_=s)
            else:
                nc.scalar.copy(out=o, in_=s)

        def quantize(codes, scales, grouped):
            nc.vector.quantize_mx(out=codes.bitcast(FP8X4), scales=scales, in_=grouped.rearrange("p c j -> p (c j)"))

        xq_sc = plane("xq_sc", 2, nc.vector)
        wq_sc = plane("wq_sc", 2, nc.vector)
        warm_bf = sbuf("warm_bf", [P, P, PACK], BF16)
        warm_codes = sbuf("warm_codes", [P, P], U32)
        warm_sc = sbuf("warm_sc", [P, P], U8)
        nc.vector.memset(warm_bf[:], 1.0)
        ws_sc = plane("ws_sc", 2, nc.vector)
        wa_sc = plane("wa_sc", 1, nc.vector)
        quantize(warm_codes[:], warm_sc[:], warm_bf[:])

        xq = [None, None]
        wq = sbuf("wq", [P, 2, 1024], U8)
        nc.sync.dma_start(out=wq[:].bitcast(I32), in_=wq_words.rearrange("z p c -> p z c").bitcast(I32))
        xq[0] = load_fp8("xq0", xq_words[0])
        for q in range(4):
            load_scale_rows(nc.sync, xq_sc, xq_scales, q)
        load_scale_rows(nc.sync, wq_sc, wq_scales, 0)
        xt_raw = load_rows("xt_raw", xt, 0, 512)
        for q in range(1, 4):
            load_scale_rows(nc.sync, wq_sc, wq_scales, q)
        xq[1] = load_fp8("xq1", xq_words[1])
        wa = sbuf("wa", [P, 1024], U8)
        nc.sync.dma_start(out=wa[:].bitcast(I32), in_=wa_words[0].bitcast(I32))
        wb_raw = [None, None]
        wb_raw[0] = load_rows("wb_raw0", wb, 0, 256)
        for q in range(4):
            load_scale_rows(nc.sync, wa_sc, wa_scales, q)
        wb_raw[1] = load_rows("wb_raw1", wb, 256, 256)
        ws = sbuf("ws", [P, 2, 512], I32)
        nc.sync.dma_start(out=ws[:], in_=ws_words.rearrange("z p c r -> p z (c r)").bitcast(I32))
        for q in range(4):
            load_scale_rows(nc.sync, ws_sc, ws_scales, q)
        wb_spans = [(0, 256), (256, 256)]

        ident = sbuf("ident", [P, P], F32)
        make_identity(nc, ident[:])
        cap_col = sbuf("cap_col", [P, 1], F32)
        nc.gpsimd.memset(cap_col[:], CAP)

        xt_codes = [sbuf("xt_codes%d" % h, [P, 256], U32) for h in range(2)]
        xt_sc = [sbuf("xt_sc%d" % h, [P, 256], U8) for h in range(2)]
        xt_bf = [sbuf("xt_bf%d" % h, [P, 256, PACK], BF16) for h in range(2)]
        wb_codes = [sbuf("wb_codes%d" % c, [P, w], U32) for c, (lo, w) in enumerate(wb_spans)]
        wb_sc = [sbuf("wb_sc%d" % c, [P, w], U8) for c, (lo, w) in enumerate(wb_spans)]
        wb_bf = [sbuf("wb_bf%d" % c, [P, w, PACK], BF16) for c, (lo, w) in enumerate(wb_spans)]

        interleave("vector", xt_bf[0][:], xt_raw[:, :, 0:256])
        interleave("scalar", xt_bf[1][:], xt_raw[:, :, 256:512])
        for h in range(2):
            quantize(xt_codes[h][:], xt_sc[h][:], xt_bf[h][:])
        interleave("vector", wb_bf[0][:], wb_raw[0][:])
        quantize(wb_codes[0][:], wb_sc[0][:], wb_bf[0][:])

        def xt_tile(i):
            h, lo = i // 2, P * (i % 2)
            return xt_codes[h][:, lo : lo + P].bitcast(FP8X4), xt_sc[h][:, lo : lo + P]

        first = [ps.tile([P, 512], F32, name="first%d" % i) for i in range(TILES)]
        second = [ps.tile([P, 512], F32, name="second%d" % i) for i in range(TILES)]

        def l_pass(bank, i, z, rhs, rhs_scale, start, stop):
            cols = slice(P * i, P * (i + 1))
            nc.tensor.matmul_mx(
                out=bank[:], lhsT=xq[z][:, cols].bitcast(FP8X4), lhsT_scale=xq_sc[:, z, cols],
                rhs=rhs, rhs_scale=rhs_scale, start=start, stop=stop,
            )

        def close_first(i):
            codes, scales = xt_tile(i)
            nc.tensor.matmul_mx(
                out=first[i][:], lhsT=codes, lhsT_scale=scales, rhs=wa[:].bitcast(FP4X4), rhs_scale=wa_sc[:, 0, :],
                start=False, stop=True,
            )

        def wb_pass(i, c):
            codes, scales = xt_tile(i)
            lo, w = wb_spans[c]
            nc.tensor.matmul_mx(
                out=second[i][:, lo : lo + w], lhsT=codes, lhsT_scale=scales,
                rhs=wb_codes[c][:].bitcast(FP8X4), rhs_scale=wb_sc[c][:], start=(c == 0), stop=False,
            )

        p_sb = [sbuf("p_sb%d" % i, [P, PACK, P], F32) for i in range(TILES)]
        gap = [sbuf("gap%d" % i, [P, PACK, P], F32) for i in range(TILES)]
        low = [sbuf("low%d" % i, [P, PACK, P], F32) for i in range(TILES)]
        high = [sbuf("high%d" % i, [P, PACK, P], F32) for i in range(TILES)]
        grown = [sbuf("grown%d" % i, [P, PACK, P], F32) for i in range(TILES)]
        soft = [sbuf("soft%d" % i, [P, PACK, P], F32) for i in range(TILES)]
        y = [sbuf("y%d" % i, [P, PACK, P], F32) for i in range(TILES)]

        def dealt(bank):
            return bank[:].rearrange("t (m r) -> t r m", r=PACK)

        def copy_first(i):
            nc.scalar.copy(out=p_sb[i][:], in_=dealt(first[i]))

        def sub(i):
            nc.vector.tensor_tensor(out=gap[i][:], in0=dealt(second[i]), in1=p_sb[i][:], op=ALU.subtract)

        def clip(i):
            if i in CLIPPED_ON_SCALAR:
                nc.scalar.activation(out=low[i][:], in_=gap[i][:], func=ACT.Relu, scale=-1.0, bias=cap_col[:])
            else:
                nc.vector.tensor_scalar(out=low[i][:], in0=gap[i][:], scalar1=CAP, scalar2=None, op0=ALU.min)

        def rest(i):
            nc.vector.scalar_tensor_tensor(
                out=high[i][:], in0=dealt(second[i]), scalar=CAP, in1=p_sb[i][:], op0=ALU.subtract, op1=ALU.max
            )

        def exp(i):
            if i in CLIPPED_ON_SCALAR:
                nc.scalar.activation(out=grown[i][:], in_=low[i][:], func=ACT.Exp, scale=-1.0, bias=cap_col[:])
            else:
                nc.scalar.activation(out=grown[i][:], in_=low[i][:], func=ACT.Exp)

        def log(i):
            nc.scalar.activation(out=soft[i][:], in_=grown[i][:], func=ACT.Ln, bias=1.0)

        def turn(i, term, opens, closes):
            for r in range(PACK):
                nc.tensor.matmul(
                    out=first[i][:, P * r : P * (r + 1)], lhsT=term[i][:, r, :], rhs=ident[:], is_transpose=True,
                    start=(opens and r == 0), stop=(closes and r == PACK - 1),
                )

        for rep in range(WARM_PASSES):
            nc.tensor.matmul_mx(
                out=second[3][:, 0:P], lhsT=warm_codes[:].bitcast(FP8X4), lhsT_scale=warm_sc[:],
                rhs=warm_codes[:].bitcast(FP8X4), rhs_scale=warm_sc[:], start=True, stop=True,
            )
        for z in range(2):
            for i in range(TILES):
                l_pass(first[i], i, z, wq[:, z, :].bitcast(FP4X4), wq_sc[:, z, :], z == 0, False)
        for i in range(TILES):
            close_first(i)
        interleave("scalar", wb_bf[1][:, 0:96], wb_raw[1][:, :, 0:96])
        interleave("vector", wb_bf[1][:, 96:256], wb_raw[1][:, :, 96:256])
        quantize(wb_codes[1][:], wb_sc[1][:], wb_bf[1][:])
        for i in range(TILES):
            copy_first(i)
        for i in range(TILES):
            wb_pass(i, 0)
        for i in range(TILES):
            wb_pass(i, 1)
            for z in range(2):
                l_pass(second[i], i, z, ws[:, z, :].bitcast(FP8X4), ws_sc[:, z, :], False, z == 1)

        for rep in range(KEEP_PASSES):
            l_pass(first[3], 3, 1, ws[:, 1, :].bitcast(FP8X4), ws_sc[:, 1, :], True, True)

        for i in range(TILES):
            sub(i)
        for i in range(TILES):
            clip(i)
        for i in range(TILES):
            exp(i)
        for i in range(TILES):
            rest(i)
            turn(i, high, True, False)
        for i in range(TILES):
            log(i)
            turn(i, soft, False, True)

        y_bf = [sbuf("y_bf0", [P, 256, PACK], BF16), sbuf("y_bf1", [P, P, PACK], BF16), sbuf("y_bf2", [P, P, PACK], BF16)]
        y_codes = sbuf("y_codes", [P, 512], U32)
        y_sc = sbuf("y_sc", [P, 512], U8)
        out_rows = out_0.rearrange("(p r) t -> p r t", r=PACK)
        out_words = out_1[0].rearrange("p c r -> p (c r)").bitcast(I32)

        for i in range(TILES):
            src = first[i][:].rearrange("p (r t) -> p r t", r=PACK)
            if i < 2:
                nc.vector.tensor_copy(out=y[i][:], in_=src)
            else:
                nc.scalar.copy(out=y[i][:], in_=src)
            nc.sync.dma_start(out=out_rows[:, :, P * i : P * (i + 1)], in_=y[i][:])
        interleave("vector", y_bf[0][:, 0:P], y[0][:])
        interleave("vector", y_bf[0][:, P : 2 * P], y[1][:])
        interleave("vector", y_bf[1][:], y[2][:])
        quantize(y_codes[:, 0:256], y_sc[:, 0:256], y_bf[0][:])
        nc.sync.dma_start(out=out_words[:, 0:256], in_=y_codes[:, 0:256].bitcast(I32))
        interleave("vector", y_bf[2][:], y[3][:])
        quantize(y_codes[:, 256:384], y_sc[:, 256:384], y_bf[1][:])
        quantize(y_codes[:, 384:512], y_sc[:, 384:512], y_bf[2][:])
        nc.sync.dma_start(out=out_words[:, 256:512], in_=y_codes[:, 256:512].bitcast(I32))
        for q in range(4):
            queue = nc.scalar if q < 2 else nc.sync
            queue.dma_start(
                out=out_2[0, 4 * q : 4 * q + 4, :].bitcast(I32),
                in_=y_sc[32 * q : 32 * q + 4, :].bitcast(I32),
            )
